import numpy as np
import ml_dtypes


def mxq(x, axis, fmt="e4m3"):
    dtype, down = {"e4m3": (ml_dtypes.float8_e4m3fn, 7), "e5m2": (ml_dtypes.float8_e5m2, 14)}[fmt]
    v = np.moveaxis(np.asarray(x, np.float32).astype(ml_dtypes.bfloat16).astype(np.float64), axis, -1)
    blocks = v.reshape(v.shape[:-1] + (-1, 32))
    amax = np.abs(blocks).max(-1, keepdims=True)
    byte = np.maximum(np.where(amax > 0, np.frexp(amax)[1] - 1 + 127, 0) - down, 1)
    scale = np.exp2(byte - 127.0)
    codes = (blocks / scale).astype(np.float32).astype(dtype).astype(np.float64)
    return np.moveaxis((codes * scale).reshape(v.shape), -1, axis)


WIDE = False


def mx_kscale(k):
    if not WIDE:
        return np.ones(k)
    levels = np.array([10, -10, 5, -5, 0])
    if k % 512:
        return np.exp2(np.random.permutation(np.resize(levels, k // 32))).repeat(32)
    a = np.empty((k // 512, 16))
    for p in range(k // 512):
        a[p, :8] = np.random.permutation(np.resize(levels, 8))
        for g in range(8):
            far = levels[np.abs(levels - a[p, g]) >= 10]
            a[p, g + 8] = far[np.random.randint(len(far))]
    return np.exp2(a.ravel()).repeat(32)


def f64(x):
    return np.asarray(x).astype(np.float64)


def striped(idx):
    return np.tile(idx.reshape(-1, 16).T, (8, 1)).astype(np.uint16)


def unstriped(offs):
    return offs[:16].T.reshape(-1).astype(np.int64)


def relu(v):
    return np.maximum(v, 0.0)


K, T, E, C, H, N = 2048, 640, 4, 128, 512, 128


def by_expert(wq, xq):
    return np.concatenate([wq[e].T @ xq[:, e * C:(e + 1) * C] for e in range(E)], axis=1)


def setup_inputs():
    n = np.random.standard_normal
    s = mx_kscale(K)[:, None]
    u = mx_kscale(H)
    return {
        "xT": (n((K, T)) * s).astype(np.float32),
        "w1": (n((E, K, H)) / np.sqrt(K) / s[None]).astype(np.float32),
        "w3": (n((E, K, H)) / np.sqrt(K) / s[None] * u[None, None, :]).astype(np.float32),
        "w2": (n((E, H, N)) / np.sqrt(H) / u[None, :, None]).astype(np.float32),
        "gate": np.tile(np.random.uniform(0.2, 1.0, E * C), (N, 1)).astype(np.float32),
        "offs": striped(np.random.permutation(T)[:E * C]),
        "dst": striped(np.random.permutation(T)[:E * C]),
    }


def reference(xT, w1, w3, w2, gate, offs, dst):
    idx = unstriped(offs)
    xq = mxq(f64(xT)[:, idx], 0, "e4m3")
    h = relu(by_expert(mxq(f64(w1), 1, "e4m3"), xq))
    h = h * by_expert(mxq(f64(w3), 1, "e4m3"), xq)
    y = by_expert(mxq(f64(w2), 1, "e4m3"), mxq(h, 0, "e4m3"))
    out = np.zeros((N, T))
    out[:, unstriped(dst)] = f64(gate) * y
    return out

@@ -1,0 +1,241 @@
+from contextlib import ExitStack
+
+import concourse.mybir as mybir
+from concourse.masks import make_identity
+
+K, T, E, C, H, N = 2048, 640, 4, 128, 512, 128
+FLOPS = 2 * E * C * (2 * K * H + H * N)
+
+F32 = mybir.dt.float32
+BF16 = mybir.dt.bfloat16
+U32 = mybir.dt.uint32
+U16 = mybir.dt.uint16
+U8 = mybir.dt.uint8
+FP8X4 = mybir.dt.float8_e4m3fn_x4
+COPY = mybir.ActivationFunctionType.Copy
+RELU = mybir.ActivationFunctionType.Relu
+MULT = mybir.AluOpType.mult
+
+P = 128
+PACK = 4
+K_PASS = P * PACK
+PASSES = K // K_PASS
+LOAD_PASSES = 2
+
+X_VECTOR = 320
+W_VECTOR = 256
+GATHER = 256
+
+
+def tile_moe_two_glu_relu_kernel(tc, xT, w1, w3, w2, gate, offs, dst, out):
+    nc = tc.nc
+    with ExitStack() as ctx:
+        keep = ctx.enter_context(tc.tile_pool(name="keep", bufs=1))
+        xraw = ctx.enter_context(tc.tile_pool(name="xraw", bufs=3))
+        xbf = ctx.enter_context(tc.tile_pool(name="xbf", bufs=2))
+        wraw = ctx.enter_context(tc.tile_pool(name="wraw", bufs=5))
+        wbf = ctx.enter_context(tc.tile_pool(name="wbf", bufs=4))
+        wq = ctx.enter_context(tc.tile_pool(name="wq", bufs=8))
+        hid = ctx.enter_context(tc.tile_pool(name="hid", bufs=2))
+        psum = ctx.enter_context(tc.psum_pool(name="psum", bufs=2))
+
+        offs_sb = keep.tile([P, E * C // 16], U16, name="offs_sb")
+        dst_sb = keep.tile([P, E * C // 16], U16, name="dst_sb")
+        nc.sync.dma_start(offs_sb[:], offs)
+
+        ident = keep.tile([P, P], F32, name="ident")
+        make_identity(nc, ident[:])
+        out_sb = keep.tile([P, T], F32, name="out_sb")
+        nc.gpsimd.memset(out_sb[:], 0.0)
+
+        gate_sb = keep.tile([P, E * C], F32, name="gate_sb")
+        w2_raw = [keep.tile([P, 2, PACK * N], F32, name=f"w2_raw{h}") for h in range(2)]
+        w2_bf = [keep.tile([P, 2, N, PACK], BF16, name=f"w2_bf{h}", align_bytes=64) for h in range(2)]
+        w2_codes = [keep.tile([P, 2 * N], U32, name=f"w2_codes{h}", align_bytes=64) for h in range(2)]
+        w2_scales = [keep.tile([P, 2 * N], U8, name=f"w2_scales{h}", align_bytes=64) for h in range(2)]
+
+        all_codes = [keep.tile([P, T], U32, name=f"all_codes{s}", align_bytes=64) for s in range(PASSES)]
+        all_scales = [keep.tile([P, T], U8, name=f"all_scales{s}", align_bytes=64) for s in range(PASSES)]
+        slot_codes = [keep.tile([P, E * C], U32, name=f"slot_codes{s}", align_bytes=64) for s in range(PASSES)]
+        slot_scales = [keep.tile([P, E * C], U8, name=f"slot_scales{s}", align_bytes=64) for s in range(PASSES)]
+        for s in range(PASSES):
+            nc.gpsimd.memset(all_scales[s][:], 0)
+
+        def load_x(s):
+            raw = xraw.tile([P, PACK * T], F32, name="x_raw")
+            nc.sync.dma_start(raw[:], xT[s * K_PASS : (s + 1) * K_PASS, :].rearrange("(p j) t -> p (j t)", j=PACK))
+            return raw
+
+        def interleave_x(raw):
+            grouped = xbf.tile([P, T, PACK], BF16, name="x_grouped", align_bytes=64)
+            rows = raw[:].rearrange("p (j t) -> p t j", j=PACK)
+            nc.vector.tensor_copy(grouped[:, :X_VECTOR, :], rows[:, :X_VECTOR, :])
+            nc.scalar.activation(grouped[:, X_VECTOR:, :], rows[:, X_VECTOR:, :], COPY)
+            return grouped
+
+        def quantize_x(s, grouped):
+            flat = grouped[:].rearrange("p t j -> p (t j)")
+            for a, b in ((0, 512), (512, T)):
+                nc.vector.quantize_mx(
+                    out=all_codes[s][:, a:b].bitcast(FP8X4),
+                    scales=all_scales[s][:, a:b],
+                    in_=flat[:, a * PACK : b * PACK],
+                )
+
+        def gather_x(s, g):
+            cols = slice(g * GATHER, (g + 1) * GATHER)
+            idx = slice(g * GATHER // 16, (g + 1) * GATHER // 16)
+            nc.vector.tensor_copy(slot_codes[s][:, cols], all_codes[s][:].indirect(offs_sb[:, idx]))
+            nc.vector.tensor_copy(slot_scales[s][:, cols], all_scales[s][:].indirect(offs_sb[:, idx]))
+
+        def load_w(w, e, half):
+            raw = wraw.tile([P, LOAD_PASSES, PACK * H], F32, name="w_raw")
+            k0 = half * LOAD_PASSES * K_PASS
+            rows = w[e, k0 : k0 + LOAD_PASSES * K_PASS, :]
+            nc.sync.dma_start(raw[:], rows.rearrange("(s p j) i -> p s (j i)", p=P, j=PACK))
+            return raw
+
+        def interleave_w(raw, r, pieces):
+            grouped = wbf.tile([P, H, PACK], BF16, name="w_grouped", align_bytes=64)
+            rows = raw[:, r, :].rearrange("p (j i) -> p i j", j=PACK)
+            width = H // pieces
+            for q in range(pieces):
+                a = q * width
+                m = a + width * W_VECTOR // H
+                b = a + width
+                nc.scalar.activation(grouped[:, m:b, :], rows[:, m:b, :], COPY)
+                nc.vector.tensor_copy(grouped[:, a:m, :], rows[:, a:m, :])
+            return grouped
+
+        def quantize_w(grouped, pieces):
+            codes = wq.tile([P, H], U32, name="w_codes", align_bytes=64)
+            scales = wq.tile([P, H], U8, name="w_scales", align_bytes=64)
+            flat = grouped[:].rearrange("p i j -> p (i j)")
+            width = H // pieces
+            for q in range(pieces):
+                a, b = q * width, (q + 1) * width
+                nc.vector.quantize_mx(
+                    out=codes[:, a:b].bitcast(FP8X4), scales=scales[:, a:b], in_=flat[:, a * PACK : b * PACK]
+                )
+            return codes, scales
+
+        def multiply_w(acc, e, s, codes, scales):
+            slots = slice(e * C, (e + 1) * C)
+            nc.tensor.matmul_mx(
+                out=acc[:],
+                lhsT=slot_codes[s][:, slots].bitcast(FP8X4),
+                lhsT_scale=slot_scales[s][:, slots],
+                rhs=codes[:].bitcast(FP8X4),
+                rhs_scale=scales[:],
+                start=(s == 0),
+                stop=(s == PASSES - 1),
+            )
+
+        def load_w2(h):
+            nc.sync.dma_start(w2_raw[h][:], w2[2 * h : 2 * h + 2].rearrange("e (p j) n -> p e (j n)", j=PACK))
+
+        def quantize_w2(h):
+            nc.scalar.activation(w2_bf[h][:], w2_raw[h][:].rearrange("p e (j n) -> p e n j", j=PACK), COPY)
+            nc.vector.quantize_mx(
+                out=w2_codes[h][:].bitcast(FP8X4),
+                scales=w2_scales[h][:],
+                in_=w2_bf[h][:].rearrange("p e n j -> p (e n j)"),
+            )
+
+        def hidden(a_acc_sb, b_acc):
+            h = hid.tile([P, H], BF16, name="h")
+            nc.vector.tensor_tensor(h[:], b_acc[:], a_acc_sb[:], MULT)
+            words = h[:].bitcast(F32)
+            turned = psum.tile([P, 2, P], F32, name="turned", bufs=1)
+            for u in range(2):
+                nc.tensor.transpose(turned[:, u, :], words[:, u : H // 2 : 2], ident[:])
+            grouped = hid.tile([P, C, PACK], BF16, name="h_grouped", align_bytes=64)
+            nc.scalar.copy(grouped[:].bitcast(F32), turned[:].rearrange("p u r -> p r u"))
+            return grouped
+
+        def quantize_h(grouped):
+            codes = hid.tile([P, C], U32, name="h_codes", align_bytes=64)
+            scales = hid.tile([P, C], U8, name="h_scales", align_bytes=64)
+            nc.vector.quantize_mx(
+                out=codes[:].bitcast(FP8X4), scales=scales[:], in_=grouped[:].rearrange("p c j -> p (c j)")
+            )
+            return codes, scales
+
+        def finish(e, codes, scales):
+            y = psum.tile([N, C], F32, name="y", bufs=1)
+            cols = slice((e % 2) * N, (e % 2 + 1) * N)
+            nc.tensor.matmul_mx(
+                out=y[:],
+                lhsT=w2_codes[e // 2][:, cols].bitcast(FP8X4),
+                lhsT_scale=w2_scales[e // 2][:, cols],
+                rhs=codes[:].bitcast(FP8X4),
+                rhs_scale=scales[:],
+                start=True,
+                stop=True,
+            )
+            y_sb = hid.tile([N, C], F32, name="y_sb")
+            nc.scalar.copy(y_sb[:], y[:])
+            idx = slice(e * C // 16, (e + 1) * C // 16)
+            nc.vector.tensor_tensor(
+                out_sb[:].indirect(dst_sb[:, idx]), y_sb[:], gate_sb[:, e * C : (e + 1) * C], MULT
+            )
+
+        raws = [load_x(s) for s in range(PASSES)]
+        nc.sync.dma_start(dst_sb[:], dst)
+        prev = None
+        for s in range(PASSES):
+            grouped = interleave_x(raws[s])
+            if prev is not None:
+                quantize_x(s - 1, prev)
+            prev = grouped
+            if s > 1:
+                gather_x(s - 2, 0)
+        quantize_x(PASSES - 1, prev)
+        gather_x(PASSES - 2, 0)
+        gather_x(PASSES - 1, 0)
+
+        chunks = [(m, e, s) for e in range(E) for m in range(2) for s in range(PASSES)]
+        last = len(chunks) - 1
+        acc = {}
+        relu_a = {}
+        waiting = {}
+        w_raw = {}
+        w_grouped = {}
+        for c in range(len(chunks) + 1):
+            if c <= last:
+                m, e, s = chunks[c]
+                if s % LOAD_PASSES == 0:
+                    w_raw[0] = load_w((w1, w3)[m], e, s // LOAD_PASSES)
+                    if e == 0 and m == 1 and s == 0:
+                        load_w2(0)
+                    if e == 0 and m == 1 and s == LOAD_PASSES:
+                        nc.sync.dma_start(gate_sb[:], gate)
+                    if c + LOAD_PASSES > last:
+                        load_w2(1)
+                w_grouped[c] = interleave_w(w_raw[0], s % LOAD_PASSES, 2 if c == last else 1)
+            if c == 0:
+                continue
+            m, e, s = chunks[c - 1]
+            codes, scales = quantize_w(w_grouped.pop(c - 1), 2 if c > last else 1)
+            if s == 0:
+                acc[m] = psum.tile([C, H], F32, name=("acc_a", "acc_b")[m])
+            multiply_w(acc[m], e, s, codes, scales)
+            if m == 0 and s == PASSES - 1:
+                relu_a[e] = hid.tile([C, H], F32, name="relu_a")
+                nc.scalar.activation(relu_a[e][:], acc[0][:], RELU)
+            if e == 0 and m == 1:
+                gather_x(s, 1)
+            if e == 1 and m == 0 and s == 0:
+                quantize_w2(0)
+            if m == 0 and s == 1 and e > 0:
+                waiting[e - 1] = quantize_h(waiting[e - 1])
+                if e - 1 < 2:
+                    finish(e - 1, *waiting[e - 1])
+            if m == 1 and s == PASSES - 1:
+                if e == E - 1:
+                    quantize_w2(1)
+                waiting[e] = hidden(relu_a[e], acc[1])
+        finish(2, *waiting[2])
+        finish(3, *quantize_h(waiting[3]))
+
+        nc.sync.dma_start(out, out_sb[:])

@@ -20,7 +20,6 @@ P = 128
 PACK = 4
 K_PASS = P * PACK
 PASSES = K // K_PASS
-LOAD_PASSES = 2
 
 X_VECTOR = 320
 W_VECTOR = 256
@@ -33,7 +32,7 @@ def tile_moe_two_glu_relu_kernel(tc, xT, w1, w3, w2, gate, offs, dst, out):
         keep = ctx.enter_context(tc.tile_pool(name="keep", bufs=1))
         xraw = ctx.enter_context(tc.tile_pool(name="xraw", bufs=3))
         xbf = ctx.enter_context(tc.tile_pool(name="xbf", bufs=2))
-        wraw = ctx.enter_context(tc.tile_pool(name="wraw", bufs=5))
+        wraw = ctx.enter_context(tc.tile_pool(name="wraw", bufs=3))
         wbf = ctx.enter_context(tc.tile_pool(name="wbf", bufs=4))
         wq = ctx.enter_context(tc.tile_pool(name="wq", bufs=8))
         hid = ctx.enter_context(tc.tile_pool(name="hid", bufs=2))
@@ -41,7 +40,6 @@ def tile_moe_two_glu_relu_kernel(tc, xT, w1, w3, w2, gate, offs, dst, out):
 
         offs_sb = keep.tile([P, E * C // 16], U16, name="offs_sb")
         dst_sb = keep.tile([P, E * C // 16], U16, name="dst_sb")
-        nc.sync.dma_start(offs_sb[:], offs)
 
         ident = keep.tile([P, P], F32, name="ident")
         make_identity(nc, ident[:])
@@ -55,11 +53,10 @@ def tile_moe_two_glu_relu_kernel(tc, xT, w1, w3, w2, gate, offs, dst, out):
         w2_scales = [keep.tile([P, 2 * N], U8, name=f"w2_scales{h}", align_bytes=64) for h in range(2)]
 
         all_codes = [keep.tile([P, T], U32, name=f"all_codes{s}", align_bytes=64) for s in range(PASSES)]
-        all_scales = [keep.tile([P, T], U8, name=f"all_scales{s}", align_bytes=64) for s in range(PASSES)]
+        all_scales = keep.tile([P, T], U8, name="all_scales", align_bytes=64)
         slot_codes = [keep.tile([P, E * C], U32, name=f"slot_codes{s}", align_bytes=64) for s in range(PASSES)]
-        slot_scales = [keep.tile([P, E * C], U8, name=f"slot_scales{s}", align_bytes=64) for s in range(PASSES)]
-        for s in range(PASSES):
-            nc.gpsimd.memset(all_scales[s][:], 0)
+        slot_scales = keep.tile([P, E * C], U8, name="slot_scales", align_bytes=64)
+        nc.gpsimd.memset(all_scales[:], 0)
 
         def load_x(s):
             raw = xraw.tile([P, PACK * T], F32, name="x_raw")
@@ -78,7 +75,7 @@ def tile_moe_two_glu_relu_kernel(tc, xT, w1, w3, w2, gate, offs, dst, out):
             for a, b in ((0, 512), (512, T)):
                 nc.vector.quantize_mx(
                     out=all_codes[s][:, a:b].bitcast(FP8X4),
-                    scales=all_scales[s][:, a:b],
+                    scales=all_scales[4 * s :, a:b],
                     in_=flat[:, a * PACK : b * PACK],
                 )
 
@@ -86,25 +83,30 @@ def tile_moe_two_glu_relu_kernel(tc, xT, w1, w3, w2, gate, offs, dst, out):
             cols = slice(g * GATHER, (g + 1) * GATHER)
             idx = slice(g * GATHER // 16, (g + 1) * GATHER // 16)
             nc.vector.tensor_copy(slot_codes[s][:, cols], all_codes[s][:].indirect(offs_sb[:, idx]))
-            nc.vector.tensor_copy(slot_scales[s][:, cols], all_scales[s][:].indirect(offs_sb[:, idx]))
+            if s == PASSES - 1:
+                nc.vector.tensor_copy(slot_scales[:, cols], all_scales[:].indirect(offs_sb[:, idx]))
 
-        def load_w(w, e, half):
-            raw = wraw.tile([P, LOAD_PASSES, PACK * H], F32, name="w_raw")
-            k0 = half * LOAD_PASSES * K_PASS
-            rows = w[e, k0 : k0 + LOAD_PASSES * K_PASS, :]
-            nc.sync.dma_start(raw[:], rows.rearrange("(s p j) i -> p s (j i)", p=P, j=PACK))
-            return raw
+        def load_w(raw, w, e, s0, s1):
+            rows = w[e, s0 * K_PASS : s1 * K_PASS, :]
+            nc.sync.dma_start(raw[:, s0:s1, :], rows.rearrange("(s p j) i -> p s (j i)", p=P, j=PACK))
 
-        def interleave_w(raw, r, pieces):
+        def load_w_rows(raw, w, e, s, j0, j1):
+            rows = w[e, s * K_PASS : (s + 1) * K_PASS, :].rearrange("(p j) i -> p j i", j=PACK)
+            cols = slice(j0 * H, j1 * H)
+            nc.sync.dma_start(
+                raw[:, s, cols].rearrange("p (j i) -> p j i", i=H), rows[:, j0:j1, :]
+            )
+
+        def interleave_w(raw, s, row_parts, col_parts):
             grouped = wbf.tile([P, H, PACK], BF16, name="w_grouped", align_bytes=64)
-            rows = raw[:, r, :].rearrange("p (j i) -> p i j", j=PACK)
-            width = H // pieces
-            for q in range(pieces):
-                a = q * width
-                m = a + width * W_VECTOR // H
-                b = a + width
-                nc.scalar.activation(grouped[:, m:b, :], rows[:, m:b, :], COPY)
-                nc.vector.tensor_copy(grouped[:, a:m, :], rows[:, a:m, :])
+            rows = raw[:, s, :].rearrange("p (j i) -> p i j", j=PACK)
+            width = H // col_parts
+            for j0, j1 in row_parts:
+                for a in range(0, H, width):
+                    m = a + width * W_VECTOR // H
+                    b = a + width
+                    nc.scalar.activation(grouped[:, m:b, j0:j1], rows[:, m:b, j0:j1], COPY)
+                    nc.vector.tensor_copy(grouped[:, a:m, j0:j1], rows[:, a:m, j0:j1])
             return grouped
 
         def quantize_w(grouped, pieces):
@@ -124,7 +126,7 @@ def tile_moe_two_glu_relu_kernel(tc, xT, w1, w3, w2, gate, offs, dst, out):
             nc.tensor.matmul_mx(
                 out=acc[:],
                 lhsT=slot_codes[s][:, slots].bitcast(FP8X4),
-                lhsT_scale=slot_scales[s][:, slots],
+                lhsT_scale=slot_scales[4 * s :, slots],
                 rhs=codes[:].bitcast(FP8X4),
                 rhs_scale=scales[:],
                 start=(s == 0),
@@ -154,33 +156,42 @@ def tile_moe_two_glu_relu_kernel(tc, xT, w1, w3, w2, gate, offs, dst, out):
             return grouped
 
         def quantize_h(grouped):
-            codes = hid.tile([P, C], U32, name="h_codes", align_bytes=64)
-            scales = hid.tile([P, C], U8, name="h_scales", align_bytes=64)
+            codes = hid.tile([P, C], U32, name="h_codes", align_bytes=64, bufs=E)
+            scales = hid.tile([P, C], U8, name="h_scales", align_bytes=64, bufs=E)
             nc.vector.quantize_mx(
                 out=codes[:].bitcast(FP8X4), scales=scales[:], in_=grouped[:].rearrange("p c j -> p (c j)")
             )
             return codes, scales
 
-        def finish(e, codes, scales):
-            y = psum.tile([N, C], F32, name="y", bufs=1)
-            cols = slice((e % 2) * N, (e % 2 + 1) * N)
-            nc.tensor.matmul_mx(
-                out=y[:],
-                lhsT=w2_codes[e // 2][:, cols].bitcast(FP8X4),
-                lhsT_scale=w2_scales[e // 2][:, cols],
-                rhs=codes[:].bitcast(FP8X4),
-                rhs_scale=scales[:],
-                start=True,
-                stop=True,
-            )
-            y_sb = hid.tile([N, C], F32, name="y_sb")
-            nc.scalar.copy(y_sb[:], y[:])
-            idx = slice(e * C // 16, (e + 1) * C // 16)
+        def project(experts):
+            first, count = experts[0], len(experts)
+            y = psum.tile([N, count, C], F32, name=f"y{count}", bufs=1)
+            for e in experts:
+                codes, scales = waiting[e]
+                cols = slice((e % 2) * N, (e % 2 + 1) * N)
+                nc.tensor.matmul_mx(
+                    out=y[:, e - first, :],
+                    lhsT=w2_codes[e // 2][:, cols].bitcast(FP8X4),
+                    lhsT_scale=w2_scales[e // 2][:, cols],
+                    rhs=codes[:].bitcast(FP8X4),
+                    rhs_scale=scales[:],
+                    start=True,
+                    stop=True,
+                )
+            y_sb = hid.tile([N, count * C], F32, name=f"y_sb{count}")
+            nc.scalar.copy(y_sb[:], y[:].rearrange("p e c -> p (e c)"))
+            return y_sb
+
+        def place(experts, y_sb):
+            first, count = experts[0], len(experts)
+            idx = slice(first * C // 16, (first + count) * C // 16)
             nc.vector.tensor_tensor(
-                out_sb[:].indirect(dst_sb[:, idx]), y_sb[:], gate_sb[:, e * C : (e + 1) * C], MULT
+                out_sb[:].indirect(dst_sb[:, idx]), y_sb[:], gate_sb[:, first * C : (first + count) * C], MULT
             )
 
-        raws = [load_x(s) for s in range(PASSES)]
+        raws = [load_x(0)]
+        nc.sync.dma_start(offs_sb[:], offs)
+        raws += [load_x(s) for s in range(1, PASSES)]
         nc.sync.dma_start(dst_sb[:], dst)
         prev = None
         for s in range(PASSES):
@@ -204,15 +215,28 @@ def tile_moe_two_glu_relu_kernel(tc, xT, w1, w3, w2, gate, offs, dst, out):
         for c in range(len(chunks) + 1):
             if c <= last:
                 m, e, s = chunks[c]
-                if s % LOAD_PASSES == 0:
-                    w_raw[0] = load_w((w1, w3)[m], e, s // LOAD_PASSES)
-                    if e == 0 and m == 1 and s == 0:
-                        load_w2(0)
-                    if e == 0 and m == 1 and s == LOAD_PASSES:
-                        nc.sync.dma_start(gate_sb[:], gate)
-                    if c + LOAD_PASSES > last:
+                w = (w1, w3)[m]
+                if s == 0:
+                    raw = wraw.tile([P, PASSES, PACK * H], F32, name="w_raw")
+                    w_raw[0] = raw
+                    if e == E - 1 and m == 1:
+                        load_w(raw, w, e, 0, 2)
+                        load_w(raw, w, e, 2, 3)
+                        load_w_rows(raw, w, e, 3, 0, 2)
+                        load_w_rows(raw, w, e, 3, 2, 4)
                         load_w2(1)
-                w_grouped[c] = interleave_w(w_raw[0], s % LOAD_PASSES, 2 if c == last else 1)
+                        nc.sync.dma_start(gate_sb[:], gate)
+                    elif e in (0, E - 1) and m == 0:
+                        load_w(raw, w, e, 0, 2)
+                        load_w(raw, w, e, 2, 4)
+                    else:
+                        load_w(raw, w, e, 0, 4)
+                    if e == 0 and m == 1:
+                        load_w2(0)
+                if c == last:
+                    w_grouped[c] = interleave_w(w_raw[0], s, ((0, 2), (2, 4)), 2)
+                else:
+                    w_grouped[c] = interleave_w(w_raw[0], s, ((0, 4),), 1)
             if c == 0:
                 continue
             m, e, s = chunks[c - 1]
@@ -225,17 +249,18 @@ def tile_moe_two_glu_relu_kernel(tc, xT, w1, w3, w2, gate, offs, dst, out):
                 nc.scalar.activation(relu_a[e][:], acc[0][:], RELU)
             if e == 0 and m == 1:
                 gather_x(s, 1)
-            if e == 1 and m == 0 and s == 0:
-                quantize_w2(0)
             if m == 0 and s == 1 and e > 0:
+                if e == 1:
+                    quantize_w2(0)
                 waiting[e - 1] = quantize_h(waiting[e - 1])
-                if e - 1 < 2:
-                    finish(e - 1, *waiting[e - 1])
+                if e == 2:
+                    y01 = project((0, 1))
             if m == 1 and s == PASSES - 1:
-                if e == E - 1:
-                    quantize_w2(1)
                 waiting[e] = hidden(relu_a[e], acc[1])
-        finish(2, *waiting[2])
-        finish(3, *quantize_h(waiting[3]))
+        place((0, 1), y01)
+        quantize_w2(1)
+        place((2,), project((2,)))
+        waiting[3] = quantize_h(waiting[3])
+        place((3,), project((3,)))
 
         nc.sync.dma_start(out, out_sb[:])

@@ -24,6 +24,7 @@ PASSES = K // K_PASS
 X_VECTOR = 320
 W_VECTOR = 256
 GATHER = 256
+WARM_UP = 3
 
 
 def tile_moe_two_glu_relu_kernel(tc, xT, w1, w3, w2, gate, offs, dst, out):
@@ -47,7 +48,8 @@ def tile_moe_two_glu_relu_kernel(tc, xT, w1, w3, w2, gate, offs, dst, out):
         nc.gpsimd.memset(out_sb[:], 0.0)
 
         gate_sb = keep.tile([P, E * C], F32, name="gate_sb")
-        w2_raw = [keep.tile([P, 2, PACK * N], F32, name=f"w2_raw{h}") for h in range(2)]
+        w2_first = keep.tile([P, 2, PACK * N], F32, name="w2_first")
+        w2_raw = {}
         w2_bf = [keep.tile([P, 2, N, PACK], BF16, name=f"w2_bf{h}", align_bytes=64) for h in range(2)]
         w2_codes = [keep.tile([P, 2 * N], U32, name=f"w2_codes{h}", align_bytes=64) for h in range(2)]
         w2_scales = [keep.tile([P, 2 * N], U8, name=f"w2_scales{h}", align_bytes=64) for h in range(2)]
@@ -86,9 +88,9 @@ def tile_moe_two_glu_relu_kernel(tc, xT, w1, w3, w2, gate, offs, dst, out):
             if s == PASSES - 1:
                 nc.vector.tensor_copy(slot_scales[:, cols], all_scales[:].indirect(offs_sb[:, idx]))
 
-        def load_w(raw, w, e, s0, s1):
+        def load_w(queue, raw, w, e, s0, s1):
             rows = w[e, s0 * K_PASS : s1 * K_PASS, :]
-            nc.sync.dma_start(raw[:, s0:s1, :], rows.rearrange("(s p j) i -> p s (j i)", p=P, j=PACK))
+            queue.dma_start(raw[:, s0:s1, :], rows.rearrange("(s p j) i -> p s (j i)", p=P, j=PACK))
 
         def load_w_rows(raw, w, e, s, j0, j1):
             rows = w[e, s * K_PASS : (s + 1) * K_PASS, :].rearrange("(p j) i -> p j i", j=PACK)
@@ -97,31 +99,24 @@ def tile_moe_two_glu_relu_kernel(tc, xT, w1, w3, w2, gate, offs, dst, out):
                 raw[:, s, cols].rearrange("p (j i) -> p j i", i=H), rows[:, j0:j1, :]
             )
 
-        def interleave_w(raw, s, row_parts, col_parts):
+        def interleave_w(raw, s, row_parts, vector_cols):
             grouped = wbf.tile([P, H, PACK], BF16, name="w_grouped", align_bytes=64)
             rows = raw[:, s, :].rearrange("p (j i) -> p i j", j=PACK)
-            width = H // col_parts
             for j0, j1 in row_parts:
-                for a in range(0, H, width):
-                    m = a + width * W_VECTOR // H
-                    b = a + width
-                    nc.scalar.activation(grouped[:, m:b, j0:j1], rows[:, m:b, j0:j1], COPY)
-                    nc.vector.tensor_copy(grouped[:, a:m, j0:j1], rows[:, a:m, j0:j1])
+                m = vector_cols
+                nc.scalar.activation(grouped[:, m:, j0:j1], rows[:, m:, j0:j1], COPY)
+                nc.vector.tensor_copy(grouped[:, :m, j0:j1], rows[:, :m, j0:j1])
             return grouped
 
-        def quantize_w(grouped, pieces):
+        def quantize_w(grouped):
             codes = wq.tile([P, H], U32, name="w_codes", align_bytes=64)
             scales = wq.tile([P, H], U8, name="w_scales", align_bytes=64)
-            flat = grouped[:].rearrange("p i j -> p (i j)")
-            width = H // pieces
-            for q in range(pieces):
-                a, b = q * width, (q + 1) * width
-                nc.vector.quantize_mx(
-                    out=codes[:, a:b].bitcast(FP8X4), scales=scales[:, a:b], in_=flat[:, a * PACK : b * PACK]
-                )
+            nc.vector.quantize_mx(
+                out=codes[:].bitcast(FP8X4), scales=scales[:], in_=grouped[:].rearrange("p i j -> p (i j)")
+            )
             return codes, scales
 
-        def multiply_w(acc, e, s, codes, scales):
+        def multiply_w(acc, e, s, codes, scales, start, stop):
             slots = slice(e * C, (e + 1) * C)
             nc.tensor.matmul_mx(
                 out=acc[:],
@@ -129,15 +124,16 @@ def tile_moe_two_glu_relu_kernel(tc, xT, w1, w3, w2, gate, offs, dst, out):
                 lhsT_scale=slot_scales[4 * s :, slots],
                 rhs=codes[:].bitcast(FP8X4),
                 rhs_scale=scales[:],
-                start=(s == 0),
-                stop=(s == PASSES - 1),
+                start=start,
+                stop=stop,
             )
 
-        def load_w2(h):
-            nc.sync.dma_start(w2_raw[h][:], w2[2 * h : 2 * h + 2].rearrange("e (p j) n -> p e (j n)", j=PACK))
+        def load_w2(h, raw):
+            w2_raw[h] = raw
+            nc.sync.dma_start(raw, w2[2 * h : 2 * h + 2].rearrange("e (p j) n -> p e (j n)", j=PACK))
 
         def quantize_w2(h):
-            nc.scalar.activation(w2_bf[h][:], w2_raw[h][:].rearrange("p e (j n) -> p e n j", j=PACK), COPY)
+            nc.scalar.activation(w2_bf[h][:], w2_raw[h].rearrange("p e (j n) -> p e n j", j=PACK), COPY)
             nc.vector.quantize_mx(
                 out=w2_codes[h][:].bitcast(FP8X4),
                 scales=w2_scales[h][:],
@@ -165,7 +161,7 @@ def tile_moe_two_glu_relu_kernel(tc, xT, w1, w3, w2, gate, offs, dst, out):
 
         def project(experts):
             first, count = experts[0], len(experts)
-            y = psum.tile([N, count, C], F32, name=f"y{count}", bufs=1)
+            y = psum.tile([N, count, C], F32, name=f"y{count}", bufs=3 - count)
             for e in experts:
                 codes, scales = waiting[e]
                 cols = slice((e % 2) * N, (e % 2 + 1) * N)
@@ -182,12 +178,9 @@ def tile_moe_two_glu_relu_kernel(tc, xT, w1, w3, w2, gate, offs, dst, out):
             nc.scalar.copy(y_sb[:], y[:].rearrange("p e c -> p (e c)"))
             return y_sb
 
-        def place(experts, y_sb):
-            first, count = experts[0], len(experts)
-            idx = slice(first * C // 16, (first + count) * C // 16)
-            nc.vector.tensor_tensor(
-                out_sb[:].indirect(dst_sb[:, idx]), y_sb[:], gate_sb[:, first * C : (first + count) * C], MULT
-            )
+        def place(e, y):
+            idx = slice(e * C // 16, (e + 1) * C // 16)
+            nc.vector.tensor_tensor(out_sb[:].indirect(dst_sb[:, idx]), y, gate_sb[:, e * C : (e + 1) * C], MULT)
 
         raws = [load_x(0)]
         nc.sync.dma_start(offs_sb[:], offs)
@@ -220,30 +213,33 @@ def tile_moe_two_glu_relu_kernel(tc, xT, w1, w3, w2, gate, offs, dst, out):
                     raw = wraw.tile([P, PASSES, PACK * H], F32, name="w_raw")
                     w_raw[0] = raw
                     if e == E - 1 and m == 1:
-                        load_w(raw, w, e, 0, 2)
-                        load_w(raw, w, e, 2, 3)
+                        load_w(nc.sync, raw, w, e, 0, 2)
+                        load_w(nc.sync, raw, w, e, 2, 3)
                         load_w_rows(raw, w, e, 3, 0, 2)
                         load_w_rows(raw, w, e, 3, 2, 4)
-                        load_w2(1)
-                        nc.sync.dma_start(gate_sb[:], gate)
-                    elif e in (0, E - 1) and m == 0:
-                        load_w(raw, w, e, 0, 2)
-                        load_w(raw, w, e, 2, 4)
+                        tail = wraw.tile([P, PASSES, PACK * H], F32, name="w_raw")
+                        load_w2(1, tail[:, 0:2, : PACK * N])
                     else:
-                        load_w(raw, w, e, 0, 4)
+                        load_w(nc.sync, raw, w, e, 0, 2)
+                        load_w(nc.scalar, raw, w, e, 2, 4)
                     if e == 0 and m == 1:
-                        load_w2(0)
+                        load_w2(0, w2_first[:])
+                        nc.sync.dma_start(gate_sb[:], gate)
                 if c == last:
-                    w_grouped[c] = interleave_w(w_raw[0], s, ((0, 2), (2, 4)), 2)
+                    w_grouped[c] = interleave_w(w_raw[0], s, ((0, 2), (2, 4)), 288)
                 else:
-                    w_grouped[c] = interleave_w(w_raw[0], s, ((0, 4),), 1)
+                    w_grouped[c] = interleave_w(w_raw[0], s, ((0, 4),), W_VECTOR)
             if c == 0:
                 continue
             m, e, s = chunks[c - 1]
-            codes, scales = quantize_w(w_grouped.pop(c - 1), 2 if c > last else 1)
+            codes, scales = quantize_w(w_grouped.pop(c - 1))
             if s == 0:
                 acc[m] = psum.tile([C, H], F32, name=("acc_a", "acc_b")[m])
-            multiply_w(acc[m], e, s, codes, scales)
+            multiply_w(acc[m], e, s, codes, scales, s == 0, s == PASSES - 1)
+            if c == last:
+                spare = psum.tile([C, H], F32, name="acc_a")
+                for repeat in range(WARM_UP):
+                    multiply_w(spare, e, s, codes, scales, True, True)
             if m == 0 and s == PASSES - 1:
                 relu_a[e] = hid.tile([C, H], F32, name="relu_a")
                 nc.scalar.activation(relu_a[e][:], acc[0][:], RELU)
@@ -255,12 +251,15 @@ def tile_moe_two_glu_relu_kernel(tc, xT, w1, w3, w2, gate, offs, dst, out):
                 waiting[e - 1] = quantize_h(waiting[e - 1])
                 if e == 2:
                     y01 = project((0, 1))
+                    place(0, y01[:, :C])
+                    place(1, y01[:, C:])
             if m == 1 and s == PASSES - 1:
                 waiting[e] = hidden(relu_a[e], acc[1])
-        place((0, 1), y01)
-        quantize_w2(1)
-        place((2,), project((2,)))
         waiting[3] = quantize_h(waiting[3])
-        place((3,), project((3,)))
+        quantize_w2(1)
+        y2 = project((2,))
+        y3 = project((3,))
+        place(2, y2[:])
+        place(3, y3[:])
 
         nc.sync.dma_start(out, out_sb[:])

@@ -221,7 +221,7 @@ def tile_moe_two_glu_relu_kernel(tc, xT, w1, w3, w2, gate, offs, dst, out):
                         load_w2(1, tail[:, 0:2, : PACK * N])
                     else:
                         load_w(nc.sync, raw, w, e, 0, 2)
-                        load_w(nc.scalar, raw, w, e, 2, 4)
+                        load_w(nc.gpsimd, raw, w, e, 2, 4)
                     if e == 0 and m == 1:
                         load_w2(0, w2_first[:])
                         nc.sync.dma_start(gate_sb[:], gate)

from contextlib import ExitStack

import concourse.mybir as mybir
from concourse.masks import make_identity

K, T, E, C, H, N = 2048, 640, 4, 128, 512, 128
FLOPS = 2 * E * C * (2 * K * H + H * N)

F32 = mybir.dt.float32
BF16 = mybir.dt.bfloat16
U32 = mybir.dt.uint32
U16 = mybir.dt.uint16
U8 = mybir.dt.uint8
FP8X4 = mybir.dt.float8_e4m3fn_x4
COPY = mybir.ActivationFunctionType.Copy
RELU = mybir.ActivationFunctionType.Relu
MULT = mybir.AluOpType.mult

P = 128
PACK = 4
K_PASS = P * PACK
PASSES = K // K_PASS

X_VECTOR = 320
W_VECTOR = 256
GATHER = 256
WARM_UP = 3


def tile_moe_two_glu_relu_kernel(tc, xT, w1, w3, w2, gate, offs, dst, out):
    nc = tc.nc
    with ExitStack() as ctx:
        keep = ctx.enter_context(tc.tile_pool(name="keep", bufs=1))
        xraw = ctx.enter_context(tc.tile_pool(name="xraw", bufs=3))
        xbf = ctx.enter_context(tc.tile_pool(name="xbf", bufs=2))
        wraw = ctx.enter_context(tc.tile_pool(name="wraw", bufs=3))
        wbf = ctx.enter_context(tc.tile_pool(name="wbf", bufs=4))
        wq = ctx.enter_context(tc.tile_pool(name="wq", bufs=8))
        hid = ctx.enter_context(tc.tile_pool(name="hid", bufs=2))
        psum = ctx.enter_context(tc.psum_pool(name="psum", bufs=2))

        offs_sb = keep.tile([P, E * C // 16], U16, name="offs_sb")
        dst_sb = keep.tile([P, E * C // 16], U16, name="dst_sb")

        ident = keep.tile([P, P], F32, name="ident")
        make_identity(nc, ident[:])
        out_sb = keep.tile([P, T], F32, name="out_sb")
        nc.gpsimd.memset(out_sb[:], 0.0)

        gate_sb = keep.tile([P, E * C], F32, name="gate_sb")
        w2_first = keep.tile([P, 2, PACK * N], F32, name="w2_first")
        w2_raw = {}
        w2_bf = [keep.tile([P, 2, N, PACK], BF16, name=f"w2_bf{h}", align_bytes=64) for h in range(2)]
        w2_codes = [keep.tile([P, 2 * N], U32, name=f"w2_codes{h}", align_bytes=64) for h in range(2)]
        w2_scales = [keep.tile([P, 2 * N], U8, name=f"w2_scales{h}", align_bytes=64) for h in range(2)]

        all_codes = [keep.tile([P, T], U32, name=f"all_codes{s}", align_bytes=64) for s in range(PASSES)]
        all_scales = keep.tile([P, T], U8, name="all_scales", align_bytes=64)
        slot_codes = [keep.tile([P, E * C], U32, name=f"slot_codes{s}", align_bytes=64) for s in range(PASSES)]
        slot_scales = keep.tile([P, E * C], U8, name="slot_scales", align_bytes=64)
        nc.gpsimd.memset(all_scales[:], 0)

        def load_x(s):
            raw = xraw.tile([P, PACK * T], F32, name="x_raw")
            nc.sync.dma_start(raw[:], xT[s * K_PASS : (s + 1) * K_PASS, :].rearrange("(p j) t -> p (j t)", j=PACK))
            return raw

        def interleave_x(raw):
            grouped = xbf.tile([P, T, PACK], BF16, name="x_grouped", align_bytes=64)
            rows = raw[:].rearrange("p (j t) -> p t j", j=PACK)
            nc.vector.tensor_copy(grouped[:, :X_VECTOR, :], rows[:, :X_VECTOR, :])
            nc.scalar.activation(grouped[:, X_VECTOR:, :], rows[:, X_VECTOR:, :], COPY)
            return grouped

        def quantize_x(s, grouped):
            flat = grouped[:].rearrange("p t j -> p (t j)")
            for a, b in ((0, 512), (512, T)):
                nc.vector.quantize_mx(
                    out=all_codes[s][:, a:b].bitcast(FP8X4),
                    scales=all_scales[4 * s :, a:b],
                    in_=flat[:, a * PACK : b * PACK],
                )

        def gather_x(s, g):
            cols = slice(g * GATHER, (g + 1) * GATHER)
            idx = slice(g * GATHER // 16, (g + 1) * GATHER // 16)
            nc.vector.tensor_copy(slot_codes[s][:, cols], all_codes[s][:].indirect(offs_sb[:, idx]))
            if s == PASSES - 1:
                nc.vector.tensor_copy(slot_scales[:, cols], all_scales[:].indirect(offs_sb[:, idx]))

        def load_w(queue, raw, w, e, s0, s1):
            rows = w[e, s0 * K_PASS : s1 * K_PASS, :]
            queue.dma_start(raw[:, s0:s1, :], rows.rearrange("(s p j) i -> p s (j i)", p=P, j=PACK))

        def load_w_rows(raw, w, e, s, j0, j1):
            rows = w[e, s * K_PASS : (s + 1) * K_PASS, :].rearrange("(p j) i -> p j i", j=PACK)
            cols = slice(j0 * H, j1 * H)
            nc.sync.dma_start(
                raw[:, s, cols].rearrange("p (j i) -> p j i", i=H), rows[:, j0:j1, :]
            )

        def interleave_w(raw, s, row_parts, vector_cols):
            grouped = wbf.tile([P, H, PACK], BF16, name="w_grouped", align_bytes=64)
            rows = raw[:, s, :].rearrange("p (j i) -> p i j", j=PACK)
            for j0, j1 in row_parts:
                m = vector_cols
                nc.scalar.activation(grouped[:, m:, j0:j1], rows[:, m:, j0:j1], COPY)
                nc.vector.tensor_copy(grouped[:, :m, j0:j1], rows[:, :m, j0:j1])
            return grouped

        def quantize_w(grouped):
            codes = wq.tile([P, H], U32, name="w_codes", align_bytes=64)
            scales = wq.tile([P, H], U8, name="w_scales", align_bytes=64)
            nc.vector.quantize_mx(
                out=codes[:].bitcast(FP8X4), scales=scales[:], in_=grouped[:].rearrange("p i j -> p (i j)")
            )
            return codes, scales

        def multiply_w(acc, e, s, codes, scales, start, stop):
            slots = slice(e * C, (e + 1) * C)
            nc.tensor.matmul_mx(
                out=acc[:],
                lhsT=slot_codes[s][:, slots].bitcast(FP8X4),
                lhsT_scale=slot_scales[4 * s :, slots],
                rhs=codes[:].bitcast(FP8X4),
                rhs_scale=scales[:],
                start=start,
                stop=stop,
            )

        def load_w2(h, raw):
            w2_raw[h] = raw
            nc.sync.dma_start(raw, w2[2 * h : 2 * h + 2].rearrange("e (p j) n -> p e (j n)", j=PACK))

        def quantize_w2(h):
            nc.scalar.activation(w2_bf[h][:], w2_raw[h].rearrange("p e (j n) -> p e n j", j=PACK), COPY)
            nc.vector.quantize_mx(
                out=w2_codes[h][:].bitcast(FP8X4),
                scales=w2_scales[h][:],
                in_=w2_bf[h][:].rearrange("p e n j -> p (e n j)"),
            )

        def hidden(a_acc_sb, b_acc):
            h = hid.tile([P, H], BF16, name="h")
            nc.vector.tensor_tensor(h[:], b_acc[:], a_acc_sb[:], MULT)
            words = h[:].bitcast(F32)
            turned = psum.tile([P, 2, P], F32, name="turned", bufs=1)
            for u in range(2):
                nc.tensor.transpose(turned[:, u, :], words[:, u : H // 2 : 2], ident[:])
            grouped = hid.tile([P, C, PACK], BF16, name="h_grouped", align_bytes=64)
            nc.scalar.copy(grouped[:].bitcast(F32), turned[:].rearrange("p u r -> p r u"))
            return grouped

        def quantize_h(grouped):
            codes = hid.tile([P, C], U32, name="h_codes", align_bytes=64, bufs=E)
            scales = hid.tile([P, C], U8, name="h_scales", align_bytes=64, bufs=E)
            nc.vector.quantize_mx(
                out=codes[:].bitcast(FP8X4), scales=scales[:], in_=grouped[:].rearrange("p c j -> p (c j)")
            )
            return codes, scales

        def project(experts):
            first, count = experts[0], len(experts)
            y = psum.tile([N, count, C], F32, name=f"y{count}", bufs=3 - count)
            for e in experts:
                codes, scales = waiting[e]
                cols = slice((e % 2) * N, (e % 2 + 1) * N)
                nc.tensor.matmul_mx(
                    out=y[:, e - first, :],
                    lhsT=w2_codes[e // 2][:, cols].bitcast(FP8X4),
                    lhsT_scale=w2_scales[e // 2][:, cols],
                    rhs=codes[:].bitcast(FP8X4),
                    rhs_scale=scales[:],
                    start=True,
                    stop=True,
                )
            y_sb = hid.tile([N, count * C], F32, name=f"y_sb{count}")
            nc.scalar.copy(y_sb[:], y[:].rearrange("p e c -> p (e c)"))
            return y_sb

        def place(e, y):
            idx = slice(e * C // 16, (e + 1) * C // 16)
            nc.vector.tensor_tensor(out_sb[:].indirect(dst_sb[:, idx]), y, gate_sb[:, e * C : (e + 1) * C], MULT)

        raws = [load_x(0)]
        nc.sync.dma_start(offs_sb[:], offs)
        raws += [load_x(s) for s in range(1, PASSES)]
        nc.sync.dma_start(dst_sb[:], dst)
        prev = None
        for s in range(PASSES):
            grouped = interleave_x(raws[s])
            if prev is not None:
                quantize_x(s - 1, prev)
            prev = grouped
            if s > 1:
                gather_x(s - 2, 0)
        quantize_x(PASSES - 1, prev)
        gather_x(PASSES - 2, 0)
        gather_x(PASSES - 1, 0)

        chunks = [(m, e, s) for e in range(E) for m in range(2) for s in range(PASSES)]
        last = len(chunks) - 1
        acc = {}
        relu_a = {}
        waiting = {}
        w_raw = {}
        w_grouped = {}
        for c in range(len(chunks) + 1):
            if c <= last:
                m, e, s = chunks[c]
                w = (w1, w3)[m]
                if s == 0:
                    raw = wraw.tile([P, PASSES, PACK * H], F32, name="w_raw")
                    w_raw[0] = raw
                    if e == E - 1 and m == 1:
                        load_w(nc.sync, raw, w, e, 0, 2)
                        load_w(nc.sync, raw, w, e, 2, 3)
                        load_w_rows(raw, w, e, 3, 0, 2)
                        load_w_rows(raw, w, e, 3, 2, 4)
                        tail = wraw.tile([P, PASSES, PACK * H], F32, name="w_raw")
                        load_w2(1, tail[:, 0:2, : PACK * N])
                    else:
                        load_w(nc.sync, raw, w, e, 0, 2)
                        load_w(nc.gpsimd, raw, w, e, 2, 4)
                    if e == 0 and m == 1:
                        load_w2(0, w2_first[:])
                        nc.sync.dma_start(gate_sb[:], gate)
                if c == last:
                    w_grouped[c] = interleave_w(w_raw[0], s, ((0, 2), (2, 4)), 288)
                else:
                    w_grouped[c] = interleave_w(w_raw[0], s, ((0, 4),), W_VECTOR)
            if c == 0:
                continue
            m, e, s = chunks[c - 1]
            codes, scales = quantize_w(w_grouped.pop(c - 1))
            if s == 0:
                acc[m] = psum.tile([C, H], F32, name=("acc_a", "acc_b")[m])
            multiply_w(acc[m], e, s, codes, scales, s == 0, s == PASSES - 1)
            if c == last:
                spare = psum.tile([C, H], F32, name="acc_a")
                for repeat in range(WARM_UP):
                    multiply_w(spare, e, s, codes, scales, True, True)
            if m == 0 and s == PASSES - 1:
                relu_a[e] = hid.tile([C, H], F32, name="relu_a")
                nc.scalar.activation(relu_a[e][:], acc[0][:], RELU)
            if e == 0 and m == 1:
                gather_x(s, 1)
            if m == 0 and s == 1 and e > 0:
                if e == 1:
                    quantize_w2(0)
                waiting[e - 1] = quantize_h(waiting[e - 1])
                if e == 2:
                    y01 = project((0, 1))
                    place(0, y01[:, :C])
                    place(1, y01[:, C:])
            if m == 1 and s == PASSES - 1:
                waiting[e] = hidden(relu_a[e], acc[1])
        waiting[3] = quantize_h(waiting[3])
        quantize_w2(1)
        y2 = project((2,))
        y3 = project((3,))
        place(2, y2[:])
        place(3, y3[:])

        nc.sync.dma_start(out, out_sb[:])
